import numpy as np
import ml_dtypes


def mxq(x, axis, fmt="e4m3"):
    dtype, down = {"e4m3": (ml_dtypes.float8_e4m3fn, 7), "e5m2": (ml_dtypes.float8_e5m2, 14)}[fmt]
    v = np.moveaxis(np.asarray(x, np.float32).astype(ml_dtypes.bfloat16).astype(np.float64), axis, -1)
    blocks = v.reshape(v.shape[:-1] + (-1, 32))
    amax = np.abs(blocks).max(-1, keepdims=True)
    byte = np.maximum(np.where(amax > 0, np.frexp(amax)[1] - 1 + 127, 0) - down, 1)
    scale = np.exp2(byte - 127.0)
    codes = (blocks / scale).astype(np.float32).astype(dtype).astype(np.float64)
    return np.moveaxis((codes * scale).reshape(v.shape), -1, axis)


WIDE = False


def mx_kscale(k):
    if not WIDE:
        return np.ones(k)
    levels = np.array([10, -10, 5, -5, 0])
    if k % 512:
        return np.exp2(np.random.permutation(np.resize(levels, k // 32))).repeat(32)
    a = np.empty((k // 512, 16))
    for p in range(k // 512):
        a[p, :8] = np.random.permutation(np.resize(levels, 8))
        for g in range(8):
            far = levels[np.abs(levels - a[p, g]) >= 10]
            a[p, g + 8] = far[np.random.randint(len(far))]
    return np.exp2(a.ravel()).repeat(32)


def f64(x):
    return np.asarray(x).astype(np.float64)


def striped(idx):
    return np.tile(idx.reshape(-1, 16).T, (8, 1)).astype(np.uint16)


def unstriped(offs):
    return offs[:16].T.reshape(-1).astype(np.int64)


E2M1 = np.array([0.0, 0.5, 1.0, 1.5, 2.0, 3.0, 4.0, 6.0, -0.0, -0.5, -1.0, -1.5, -2.0, -3.0, -4.0, -6.0])


def pack_weight(w, fmt):
    k, n = w.shape
    w = f64(np.asarray(w, np.float32).astype(ml_dtypes.bfloat16)).reshape(k // 32, 32, n)
    amax = np.abs(w).max(1)
    if fmt == "e4m3":
        byte = np.frexp(amax)[1] - 1 + 127 - 7
    else:
        mant, ex = np.frexp(amax / 6.0)
        byte = np.where(mant > 0.5, ex, ex - 1) + 127
    byte = np.clip(np.where(amax > 0, byte, 1), 1, 254)
    scaled = (w * np.exp2(127.0 - byte)[:, None, :]).reshape(k, n).astype(np.float32)
    by_word = np.ascontiguousarray(scaled.reshape(k // 512, 128, 4, n).transpose(0, 1, 3, 2))
    if fmt == "e4m3":
        words = by_word.astype(ml_dtypes.float8_e4m3fn).view(np.uint8)
    else:
        c = by_word.astype(ml_dtypes.float4_e2m1fn).view(np.uint8) & 0xF
        words = (c[..., 0::2] | (c[..., 1::2] << 4)).reshape(k // 512, 128, 2 * n)
    return np.ascontiguousarray(words), np.ascontiguousarray(byte.astype(np.uint8).reshape(k // 512, 16, n))


def unpack_weight(words, scales, fmt):
    g, _, n = scales.shape
    words = np.ascontiguousarray(words).reshape(g, 128, n, -1)
    if fmt == "e4m3":
        vals = words.view(ml_dtypes.float8_e4m3fn).astype(np.float64)
    else:
        nib = np.empty((g, 128, n, 4), np.uint8)
        nib[..., 0::2] = words & 0xF
        nib[..., 1::2] = words >> 4
        vals = E2M1[nib]
    vals = vals * np.repeat(np.exp2(scales.astype(np.float64) - 127.0), 8, axis=1)[..., None]
    return vals.transpose(0, 1, 3, 2).reshape(g * 512, n)


def relu(v):
    return np.maximum(v, 0.0)


K, T, Q, E, C, D, H = 512, 512, 1024, 8, 128, 128, 512
N = 128


def by_expert(wq, xq, C):
    return np.concatenate([wq[e].T @ xq[:, e * C:(e + 1) * C] for e in range(E)], axis=1)


def setup_inputs():
    n = np.random.standard_normal
    s = mx_kscale(K)
    u = mx_kscale(H)
    first = np.random.permutation(np.repeat(np.arange(E), T // E))
    second = (first + 1 + np.random.permutation(np.repeat(np.arange(E - 1), -(-T // (E - 1)))[:T])) % E
    while np.bincount(second, minlength=E).max() != T // E:
        load = np.bincount(second, minlength=E); hi, lo = int(load.argmax()), int(load.argmin())
        t = np.flatnonzero((second == hi) & (first != lo))[0]; second[t] = lo
    slot_token = np.empty(E * C, np.int64); pos = np.empty((2, T), np.int64); fill = np.zeros(E, np.int64)
    place = np.stack([np.random.permutation(C) for _ in range(E)])
    for r, deal in enumerate((first, second)):
        for t in np.random.permutation(T):
            e = deal[t]; j = e * C + place[e, fill[e]]; fill[e] += 1; slot_token[j] = t; pos[r, t] = j
    g = np.random.uniform(0.2, 0.8, T)
    slots2 = np.concatenate([np.random.permutation(Q)[:D] for e in range(E)])
    x = pack_weight(n((K, Q)) * s[:, None], "e4m3")
    w1 = [pack_weight(m, "e2m1") for m in n((E, K, H)) / np.sqrt(K) / s[None, :, None]]
    w3 = [pack_weight(m, "e2m1") for m in n((E, K, H)) / np.sqrt(K) / s[None, :, None] * u]
    w2 = [pack_weight(m, "e2m1") for m in n((E, H, N)) / np.sqrt(H) / u[None, :, None]]
    return {
        "x_words": x[0],
        "x_scales": x[1],
        "xo": (n((K, T)) * s[:, None]).astype(np.float32),
        "w1_words": np.stack([m[0] for m in w1]),
        "w1_scales": np.stack([m[1] for m in w1]),
        "w3_words": np.stack([m[0] for m in w3]),
        "w3_scales": np.stack([m[1] for m in w3]),
        "w2_words": np.stack([m[0] for m in w2]),
        "w2_scales": np.stack([m[1] for m in w2]),
        "gate": np.stack([np.tile(g, (128, 1)), np.tile(1.0 - g, (128, 1))]).astype(np.float32),
        "offs": striped(slot_token),
        "pos1": striped(pos[0]),
        "pos2": striped(pos[1]),
        "offs2": striped(slots2),
    }


def reference(x_words, x_scales, xo, w1_words, w1_scales, w3_words, w3_scales, w2_words, w2_scales, gate, offs, pos1, pos2, offs2):
    w1 = np.stack([unpack_weight(w1_words[e], w1_scales[e], "e2m1") for e in range(E)])
    w3 = np.stack([unpack_weight(w3_words[e], w3_scales[e], "e2m1") for e in range(E)])
    w2 = np.stack([unpack_weight(w2_words[e], w2_scales[e], "e2m1") for e in range(E)])
    idx, idx2 = unstriped(offs), unstriped(offs2)
    xq = mxq(f64(xo)[:, idx], 0, "e4m3")
    rq = unpack_weight(x_words, x_scales, "e4m3")[:, idx2]
    h = relu(by_expert(w1, xq, C)) * by_expert(w3, xq, C)
    y = by_expert(w2, mxq(h, 0, "e4m3"), C)
    h = relu(by_expert(w1, rq, D)) * by_expert(w3, rq, D)
    z = by_expert(w2, mxq(h, 0, "e4m3"), D)
    own = sum(f64(gate[r, :1]) * y[:, unstriped(p)] for r, p in enumerate((pos1, pos2)))
    return np.concatenate([own, z], axis=1)

@@ -1,0 +1,213 @@
+from contextlib import ExitStack
+
+import concourse.mybir as mybir
+from concourse.masks import make_identity
+
+K, T, Q, E, C, H, N = 512, 512, 1024, 8, 128, 512, 128
+FLOPS = 2 * (2 * E * C) * (2 * K * H + H * N)
+
+F32 = mybir.dt.float32
+BF16 = mybir.dt.bfloat16
+I32 = mybir.dt.int32
+U32 = mybir.dt.uint32
+U16 = mybir.dt.uint16
+U8 = mybir.dt.uint8
+FP8X4 = mybir.dt.float8_e4m3fn_x4
+FP4X4 = mybir.dt.float4_e2m1fn_x4
+MULT = mybir.AluOpType.mult
+ADD = mybir.AluOpType.add
+RELU = mybir.ActivationFunctionType.Relu
+
+P = 128
+PAIR = 2
+S = PAIR * C
+LCOL = S // 16
+UNITS = [("far", 0), ("far", 1), ("own", 0), ("own", 1), ("own", 2), ("own", 3), ("far", 2), ("far", 3)]
+
+
+def tile_moe_loc_glu_relu_kernel(tc, x_words, x_scales, xo, w1_words, w1_scales, w3_words, w3_scales, w2_words, w2_scales, gate, offs, pos1, pos2, offs2, out):
+    nc = tc.nc
+    with ExitStack() as ctx:
+        lists = ctx.enter_context(tc.tile_pool(name="lists", bufs=1))
+        keep = ctx.enter_context(tc.tile_pool(name="keep", bufs=1))
+        work = ctx.enter_context(tc.tile_pool(name="work", bufs=3))
+        psum = ctx.enter_context(tc.psum_pool(name="psum", bufs=1))
+
+        own_list = lists.tile([P, E * C // 16], U16, name="own_list")
+        far_list = lists.tile([P, E * C // 16], U16, name="far_list")
+        pos_lists = [lists.tile([P, T // 16], U16, name="pos_list%d" % r) for r in range(2)]
+
+        far_words = keep.tile([P, Q], I32, name="far_words", align_bytes=64)
+        far_bytes = keep.tile([P, Q], U8, name="far_bytes", align_bytes=64)
+        w1_plane = keep.tile([P, E, H], U8, name="w1_plane", align_bytes=64)
+        w3_plane = keep.tile([P, E, H], U8, name="w3_plane", align_bytes=64)
+        w2_plane = keep.tile([P, E, N], U8, name="w2_plane", align_bytes=64)
+        w1_sb = [keep.tile([P, PAIR, 2 * H], U8, name="w1_sb%d" % j, align_bytes=64) for j in range(E // PAIR)]
+        w3_sb = [keep.tile([P, PAIR, 2 * H], U8, name="w3_sb%d" % j, align_bytes=64) for j in range(E // PAIR)]
+        w2_sb = keep.tile([P, E, 2 * N], U8, name="w2_sb", align_bytes=64)
+        xo_raw = [keep.tile([P, 2, T], F32, name="xo_raw%d" % u) for u in range(2)]
+        xo_pairs = [keep.tile([P, T, 2], BF16, name="xo_pairs%d" % u, align_bytes=64) for u in range(2)]
+        gate_sb = keep.tile([P, 2, T], F32, name="gate_sb")
+        y_own = keep.tile([P, E * C], F32, name="y_own")
+        ident = keep.tile([P, P], F32, name="ident")
+
+        nc.vector.memset(far_bytes[:].bitcast(I32), 0)
+        nc.vector.memset(w1_plane[:].bitcast(I32), 0)
+        nc.vector.memset(w3_plane[:].bitcast(I32), 0)
+        nc.vector.memset(w2_plane[:].bitcast(I32), 0)
+        make_identity(nc, ident[:])
+
+        def load_plane(plane, scales):
+            for q in range(4):
+                nc.sync.dma_start(
+                    out=plane[32 * q : 32 * q + 4].bitcast(I32),
+                    in_=scales[:, 0, 4 * q : 4 * q + 4, :].rearrange("e b i -> b e i").bitcast(I32),
+                )
+
+        def load_words(dst, words, first, count):
+            nc.sync.dma_start(
+                out=dst[:].bitcast(I32),
+                in_=words[first : first + count, 0].rearrange("e p c -> p e c").bitcast(I32),
+            )
+
+        xo_rows = xo.rearrange("(p j) t -> p j t", j=4)
+
+        nc.sync.dma_start(far_list[:], offs2)
+        nc.sync.dma_start(out=far_words[:], in_=x_words[0].rearrange("p n d -> p (n d)").bitcast(I32))
+        nc.sync.dma_start(out=xo_raw[0][:], in_=xo_rows[:, 0:2, :])
+        for q in range(4):
+            nc.sync.dma_start(out=far_bytes[32 * q : 32 * q + 4].bitcast(I32), in_=x_scales[0, 4 * q : 4 * q + 4, :].bitcast(I32))
+        nc.sync.dma_start(out=xo_raw[1][:], in_=xo_rows[:, 2:4, :])
+        nc.sync.dma_start(own_list[:], offs)
+        load_words(w1_sb[0], w1_words, 0, PAIR)
+        load_words(w3_sb[0], w3_words, 0, PAIR)
+        load_plane(w1_plane, w1_scales)
+        load_plane(w3_plane, w3_scales)
+        load_words(w1_sb[1], w1_words, PAIR, PAIR)
+        load_words(w3_sb[1], w3_words, PAIR, PAIR)
+        load_words(w2_sb, w2_words, 0, E)
+        load_plane(w2_plane, w2_scales)
+        for j in range(2, E // PAIR):
+            load_words(w1_sb[j], w1_words, PAIR * j, PAIR)
+            load_words(w3_sb[j], w3_words, PAIR * j, PAIR)
+        nc.sync.dma_start(pos_lists[0][:], pos1)
+        nc.sync.dma_start(pos_lists[1][:], pos2)
+        nc.sync.dma_start(out=gate_sb[:], in_=gate.rearrange("r p t -> p r t"))
+
+        x_mx = {}
+        h_rows = {}
+        h_mx = {}
+
+        def cast_own_tokens():
+            for u in range(2):
+                nc.scalar.copy(out=xo_pairs[u][:], in_=xo_raw[u][:].rearrange("p e t -> p t e"))
+
+        def gather(n):
+            kind, j = UNITS[n]
+            codes = keep.tile([P, S], U32, name="x_codes%d" % n, align_bytes=64)
+            scales = keep.tile([P, S], U8, name="x_bytes%d" % n, align_bytes=64)
+            x_mx[n] = (codes, scales)
+            cols = slice(j * LCOL, (j + 1) * LCOL)
+            if kind == "far":
+                nc.vector.tensor_copy(codes[:], far_words[:].bitcast(U32).indirect(far_list[:, cols]))
+                nc.vector.tensor_copy(scales[:], far_bytes[:].indirect(far_list[:, cols]))
+                return
+            picked = work.tile([P, 2, S, 2], BF16, name="picked", align_bytes=64)
+            for u in range(2):
+                nc.vector.tensor_copy(
+                    picked[:, u].rearrange("p s e -> p (s e)").bitcast(U32),
+                    xo_pairs[u][:].rearrange("p t e -> p (t e)").bitcast(U32).indirect(own_list[:, cols]),
+                )
+            grouped = work.tile([P, S, 2, 2], BF16, name="x_grouped", align_bytes=64)
+            nc.scalar.copy(out=grouped[:], in_=picked[:].rearrange("p u s e -> p s u e"))
+            nc.vector.quantize_mx(out=codes[:].bitcast(FP8X4), scales=scales[:], in_=grouped[:].rearrange("p s u e -> p (s u e)"))
+
+        def first_layer(n):
+            kind, j = UNITS[n]
+            codes, scales = x_mx[n]
+            h_rows[n] = []
+            for i in range(PAIR):
+                slots = slice(i * C, (i + 1) * C)
+                a = psum.tile([P, H], F32, name="a_bank", bufs=2)
+                b = psum.tile([P, H], F32, name="b_bank", bufs=3)
+                for bank, w_sb, plane in ((a, w1_sb, w1_plane), (b, w3_sb, w3_plane)):
+                    nc.tensor.matmul_mx(
+                        out=bank[:],
+                        lhsT=codes[:, slots].bitcast(FP8X4),
+                        lhsT_scale=scales[:, slots],
+                        rhs=w_sb[j][:, i, :].bitcast(FP4X4),
+                        rhs_scale=plane[:, PAIR * j + i, :],
+                        start=True,
+                        stop=True,
+                    )
+                relu_a = work.tile([P, 2, P, 2], F32, name="relu_a")
+                nc.scalar.activation(relu_a[:], a[:].rearrange("s (p u e) -> s u p e", u=2, e=2), RELU)
+                h = work.tile([P, 2, P, 2], BF16, name="h_rows", bufs=4, align_bytes=64)
+                nc.vector.tensor_tensor(h[:], relu_a[:], b[:].rearrange("s (p u e) -> s u p e", u=2, e=2), MULT)
+                h_rows[n].append(h)
+
+        def turn(n):
+            turned = psum.tile([P, PAIR, 2, C], F32, name="turned", bufs=2)
+            for i in range(PAIR):
+                for u in range(2):
+                    nc.tensor.transpose(turned[:, i, u, :], h_rows[n][i][:, u].rearrange("s p e -> s (p e)").bitcast(F32), ident[:])
+            grouped = work.tile([P, S * 4], BF16, name="h_grouped", align_bytes=64)
+            nc.scalar.copy(
+                out=grouped[:].bitcast(F32).rearrange("p (i s u) -> p i s u", i=PAIR, u=2),
+                in_=turned[:].rearrange("p i u s -> p i s u"),
+            )
+            codes = work.tile([P, S], U32, name="h_codes", align_bytes=64)
+            scales = work.tile([P, S], U8, name="h_bytes", align_bytes=64)
+            nc.vector.quantize_mx(out=codes[:].bitcast(FP8X4), scales=scales[:], in_=grouped[:])
+            h_mx[n] = (codes, scales)
+
+        def second_layer(n):
+            kind, j = UNITS[n]
+            codes, scales = h_mx[n]
+            y = psum.tile([P, S], F32, name="y_bank", bufs=1)
+            for i in range(PAIR):
+                slots = slice(i * C, (i + 1) * C)
+                nc.tensor.matmul_mx(
+                    out=y[:, slots],
+                    lhsT=w2_sb[:, PAIR * j + i, :].bitcast(FP4X4),
+                    lhsT_scale=w2_plane[:, PAIR * j + i, :],
+                    rhs=codes[:, slots].bitcast(FP8X4),
+                    rhs_scale=scales[:, slots],
+                    start=True,
+                    stop=True,
+                )
+            if kind == "own":
+                nc.scalar.copy(out=y_own[:, j * S : (j + 1) * S], in_=y[:])
+                return
+            z = work.tile([P, S], F32, name="z")
+            nc.scalar.copy(out=z[:], in_=y[:])
+            nc.sync.dma_start(out=out[:, T + j * S : T + (j + 1) * S], in_=z[:])
+
+        def combine(half):
+            tokens = slice(half * S, (half + 1) * S)
+            parts = []
+            for r in range(2):
+                part = work.tile([P, S], F32, name="part", bufs=4)
+                nc.vector.tensor_tensor(
+                    part[:], y_own[:].indirect(pos_lists[r][:, half * LCOL : (half + 1) * LCOL]), gate_sb[:, r, tokens], MULT
+                )
+                parts.append(part)
+            total = work.tile([P, S], F32, name="total")
+            nc.vector.tensor_tensor(total[:], parts[0][:], parts[1][:], ADD)
+            nc.sync.dma_start(out=out[:, tokens], in_=total[:])
+
+        count = len(UNITS)
+        gather(0)
+        gather(1)
+        cast_own_tokens()
+        for step in range(count + 2):
+            if step < count:
+                first_layer(step)
+            if 1 <= step <= count:
+                turn(step - 1)
+            if step >= 2:
+                second_layer(step - 2)
+            if step + 2 < count:
+                gather(step + 2)
+        combine(0)
+        combine(1)

@@ -22,7 +22,11 @@ P = 128
 PAIR = 2
 S = PAIR * C
 LCOL = S // 16
-UNITS = [("far", 0), ("far", 1), ("own", 0), ("own", 1), ("own", 2), ("own", 3), ("far", 2), ("far", 3)]
+UNITS = [("far", 0), ("own", 0), ("own", 1), ("own", 2), ("own", 3), ("far", 1), ("far", 2), ("far", 3)]
+REUSES = {"pk4": "r01", "xg3": "r00", "xg4": "r11", "s5": "r21", "s6": "r30", "s7": "r40", "pt10": "hg6", "pt11": "hg7", "pt00": "r71"}
+LOADS = "fl fw xr0 xs xr1 ol w3_0 w3s w1s w1_0 w2 w2s w1_1 w3_1 w1_2 w3_2 w1_3 w3_3 p0 p1 gate".split()
+ORDER = "cast gw0 gb0 gw5 gw6 gw7 go1 il1 qx1 go2 il2 qx2 go3 F0 go4 il3 qx3 F1 T0 il4 qx4 F2 T1 S0 gb5 F3 T2 S1 gb6 F4 T3 S2 gb7 F5 T4 S3 F6 S4 T5 F7 T6 S5 T7 S6 S7 C0 C1".split()
+STEPPED = False
 
 
 def tile_moe_loc_glu_relu_kernel(tc, x_words, x_scales, xo, w1_words, w1_scales, w3_words, w3_scales, w2_words, w2_scales, gate, offs, pos1, pos2, offs2, out):
@@ -31,6 +35,7 @@ def tile_moe_loc_glu_relu_kernel(tc, x_words, x_scales, xo, w1_words, w1_scales,
         lists = ctx.enter_context(tc.tile_pool(name="lists", bufs=1))
         keep = ctx.enter_context(tc.tile_pool(name="keep", bufs=1))
         work = ctx.enter_context(tc.tile_pool(name="work", bufs=3))
+        placed = ctx.enter_context(tc.tile_pool(name="placed", bufs=1))
         psum = ctx.enter_context(tc.psum_pool(name="psum", bufs=1))
 
         own_list = lists.tile([P, E * C // 16], U16, name="own_list")
@@ -52,16 +57,16 @@ def tile_moe_loc_glu_relu_kernel(tc, x_words, x_scales, xo, w1_words, w1_scales,
         ident = keep.tile([P, P], F32, name="ident")
 
         nc.vector.memset(far_bytes[:].bitcast(I32), 0)
-        nc.vector.memset(w1_plane[:].bitcast(I32), 0)
+        nc.gpsimd.memset(w1_plane[:].bitcast(I32), 0)
         nc.vector.memset(w3_plane[:].bitcast(I32), 0)
         nc.vector.memset(w2_plane[:].bitcast(I32), 0)
         make_identity(nc, ident[:])
 
         def load_plane(plane, scales):
-            for q in range(4):
+            for r in range(4):
                 nc.sync.dma_start(
-                    out=plane[32 * q : 32 * q + 4].bitcast(I32),
-                    in_=scales[:, 0, 4 * q : 4 * q + 4, :].rearrange("e b i -> b e i").bitcast(I32),
+                    out=plane[r:P:32].bitcast(I32),
+                    in_=scales[:, 0].rearrange("e (q r) i -> r q e i", r=4)[r].bitcast(I32),
                 )
 
         def load_words(dst, words, first, count):
@@ -72,29 +77,42 @@ def tile_moe_loc_glu_relu_kernel(tc, x_words, x_scales, xo, w1_words, w1_scales,
 
         xo_rows = xo.rearrange("(p j) t -> p j t", j=4)
 
-        nc.sync.dma_start(far_list[:], offs2)
-        nc.sync.dma_start(out=far_words[:], in_=x_words[0].rearrange("p n d -> p (n d)").bitcast(I32))
-        nc.sync.dma_start(out=xo_raw[0][:], in_=xo_rows[:, 0:2, :])
-        for q in range(4):
-            nc.sync.dma_start(out=far_bytes[32 * q : 32 * q + 4].bitcast(I32), in_=x_scales[0, 4 * q : 4 * q + 4, :].bitcast(I32))
-        nc.sync.dma_start(out=xo_raw[1][:], in_=xo_rows[:, 2:4, :])
-        nc.sync.dma_start(own_list[:], offs)
-        load_words(w1_sb[0], w1_words, 0, PAIR)
-        load_words(w3_sb[0], w3_words, 0, PAIR)
-        load_plane(w1_plane, w1_scales)
-        load_plane(w3_plane, w3_scales)
-        load_words(w1_sb[1], w1_words, PAIR, PAIR)
-        load_words(w3_sb[1], w3_words, PAIR, PAIR)
-        load_words(w2_sb, w2_words, 0, E)
-        load_plane(w2_plane, w2_scales)
-        for j in range(2, E // PAIR):
-            load_words(w1_sb[j], w1_words, PAIR * j, PAIR)
-            load_words(w3_sb[j], w3_words, PAIR * j, PAIR)
-        nc.sync.dma_start(pos_lists[0][:], pos1)
-        nc.sync.dma_start(pos_lists[1][:], pos2)
-        nc.sync.dma_start(out=gate_sb[:], in_=gate.rearrange("r p t -> p r t"))
+        def load(name):
+            if name in ("fl", "ol", "p0", "p1"):
+                dst, src = {"fl": (far_list, offs2), "ol": (own_list, offs), "p0": (pos_lists[0], pos1), "p1": (pos_lists[1], pos2)}[name]
+                nc.sync.dma_start(dst[:], src)
+            elif name == "fw":
+                nc.sync.dma_start(out=far_words[:], in_=x_words[0].rearrange("p n d -> p (n d)").bitcast(I32))
+            elif name in ("xr0", "xr1"):
+                u = int(name[2])
+                nc.sync.dma_start(out=xo_raw[u][:], in_=xo_rows[:, 2 * u : 2 * u + 2, :])
+            elif name == "xs":
+                for r in range(4):
+                    nc.sync.dma_start(out=far_bytes[r:P:32].bitcast(I32), in_=x_scales[0].rearrange("(q r) n -> r q n", r=4)[r].bitcast(I32))
+            elif name in ("w1s", "w3s", "w2s"):
+                load_plane(*{"w1s": (w1_plane, w1_scales), "w3s": (w3_plane, w3_scales), "w2s": (w2_plane, w2_scales)}[name])
+            elif name == "w2":
+                load_words(w2_sb, w2_words, 0, E)
+            elif name == "gate":
+                nc.sync.dma_start(out=gate_sb[:], in_=gate.rearrange("r p t -> p r t"))
+            else:
+                j = int(name[3])
+                load_words((w1_sb if name[1] == "1" else w3_sb)[j], w1_words if name[1] == "1" else w3_words, PAIR * j, PAIR)
 
-        x_mx = {}
+        for name in LOADS:
+            load(name)
+
+        SLOT = 2048
+        offsets = {"r%d%d" % (n, i): SLOT * (2 * n + i) for n in range(8) for i in range(2)}
+        for n in range(8):
+            offsets["hg%d" % n] = SLOT * (16 + n)
+
+        def new_tile(name, shape, dtype):
+            home = REUSES.get(name, name)
+            if home in offsets:
+                return placed.tile(shape, dtype, name=name, align_bytes=64, offset=offsets[home])
+            return keep.tile(shape, dtype, name=name, align_bytes=64)
+
         h_rows = {}
         h_mx = {}
 
@@ -102,34 +120,55 @@ def tile_moe_loc_glu_relu_kernel(tc, x_words, x_scales, xo, w1_words, w1_scales,
             for u in range(2):
                 nc.scalar.copy(out=xo_pairs[u][:], in_=xo_raw[u][:].rearrange("p e t -> p t e"))
 
-        def gather(n):
-            kind, j = UNITS[n]
-            codes = keep.tile([P, S], U32, name="x_codes%d" % n, align_bytes=64)
-            scales = keep.tile([P, S], U8, name="x_bytes%d" % n, align_bytes=64)
-            x_mx[n] = (codes, scales)
-            cols = slice(j * LCOL, (j + 1) * LCOL)
-            if kind == "far":
-                nc.vector.tensor_copy(codes[:], far_words[:].bitcast(U32).indirect(far_list[:, cols]))
-                nc.vector.tensor_copy(scales[:], far_bytes[:].indirect(far_list[:, cols]))
-                return
-            picked = work.tile([P, 2, S, 2], BF16, name="picked", align_bytes=64)
+        x_codes = {}
+        x_bytes = {}
+        picked = {}
+        x_grouped = {}
+
+        def list_cols(n):
+            j = UNITS[n][1]
+            return slice(j * LCOL, (j + 1) * LCOL)
+
+        def gather_words(n):
+            x_codes[n] = new_tile("c%d" % n, [P, S], U32)
+            nc.vector.tensor_copy(x_codes[n][:], far_words[:].bitcast(U32).indirect(far_list[:, list_cols(n)]))
+
+        def gather_bytes(n):
+            x_bytes[n] = new_tile("s%d" % n, [P, S], U8)
+            nc.vector.tensor_copy(x_bytes[n][:], far_bytes[:].indirect(far_list[:, list_cols(n)]))
+
+        def gather_own(n):
+            if STEPPED:
+                x_grouped[n] = new_tile("xg%d" % n, [P, S * 4], BF16)
+                dst = [x_grouped[n][:].bitcast(U32).rearrange("p (s u) -> p s u", u=2)[:, :, u] for u in range(2)]
+            else:
+                picked[n] = new_tile("pk%d" % n, [P, 2, S * 2], BF16)
+                dst = [picked[n][:, u].bitcast(U32) for u in range(2)]
             for u in range(2):
-                nc.vector.tensor_copy(
-                    picked[:, u].rearrange("p s e -> p (s e)").bitcast(U32),
-                    xo_pairs[u][:].rearrange("p t e -> p (t e)").bitcast(U32).indirect(own_list[:, cols]),
-                )
-            grouped = work.tile([P, S, 2, 2], BF16, name="x_grouped", align_bytes=64)
-            nc.scalar.copy(out=grouped[:], in_=picked[:].rearrange("p u s e -> p s u e"))
-            nc.vector.quantize_mx(out=codes[:].bitcast(FP8X4), scales=scales[:], in_=grouped[:].rearrange("p s u e -> p (s u e)"))
+                nc.vector.tensor_copy(dst[u], xo_pairs[u][:].rearrange("p t e -> p (t e)").bitcast(U32).indirect(own_list[:, list_cols(n)]))
+
+        def interleave(n):
+            if STEPPED:
+                return
+            x_grouped[n] = new_tile("xg%d" % n, [P, S * 4], BF16)
+            nc.scalar.copy(
+                out=x_grouped[n][:].rearrange("p (s u e) -> p s u e", u=2, e=2),
+                in_=picked[n][:].rearrange("p u (s e) -> p s u e", e=2),
+            )
+
+        def quantize_own(n):
+            x_codes[n] = new_tile("c%d" % n, [P, S], U32)
+            x_bytes[n] = new_tile("s%d" % n, [P, S], U8)
+            nc.vector.quantize_mx(out=x_codes[n][:].bitcast(FP8X4), scales=x_bytes[n][:], in_=x_grouped[n][:])
 
         def first_layer(n):
             kind, j = UNITS[n]
-            codes, scales = x_mx[n]
+            codes, scales = x_codes[n], x_bytes[n]
             h_rows[n] = []
             for i in range(PAIR):
                 slots = slice(i * C, (i + 1) * C)
-                a = psum.tile([P, H], F32, name="a_bank", bufs=2)
-                b = psum.tile([P, H], F32, name="b_bank", bufs=3)
+                a = psum.tile([P, H], F32, name="a_bank", bufs=3)
+                b = psum.tile([P, H], F32, name="b_bank", bufs=2)
                 for bank, w_sb, plane in ((a, w1_sb, w1_plane), (b, w3_sb, w3_plane)):
                     nc.tensor.matmul_mx(
                         out=bank[:],
@@ -140,7 +179,7 @@ def tile_moe_loc_glu_relu_kernel(tc, x_words, x_scales, xo, w1_words, w1_scales,
                         start=True,
                         stop=True,
                     )
-                relu_a = work.tile([P, 2, P, 2], F32, name="relu_a")
+                relu_a = new_tile("r%d%d" % (n, i), [P, 2, P, 2], F32)
                 nc.scalar.activation(relu_a[:], a[:].rearrange("s (p u e) -> s u p e", u=2, e=2), RELU)
                 h = work.tile([P, 2, P, 2], BF16, name="h_rows", bufs=4, align_bytes=64)
                 nc.vector.tensor_tensor(h[:], relu_a[:], b[:].rearrange("s (p u e) -> s u p e", u=2, e=2), MULT)
@@ -151,7 +190,7 @@ def tile_moe_loc_glu_relu_kernel(tc, x_words, x_scales, xo, w1_words, w1_scales,
             for i in range(PAIR):
                 for u in range(2):
                     nc.tensor.transpose(turned[:, i, u, :], h_rows[n][i][:, u].rearrange("s p e -> s (p e)").bitcast(F32), ident[:])
-            grouped = work.tile([P, S * 4], BF16, name="h_grouped", align_bytes=64)
+            grouped = new_tile("hg%d" % n, [P, S * 4], BF16)
             nc.scalar.copy(
                 out=grouped[:].bitcast(F32).rearrange("p (i s u) -> p i s u", i=PAIR, u=2),
                 in_=turned[:].rearrange("p i u s -> p i s u"),
@@ -187,7 +226,7 @@ def tile_moe_loc_glu_relu_kernel(tc, x_words, x_scales, xo, w1_words, w1_scales,
             tokens = slice(half * S, (half + 1) * S)
             parts = []
             for r in range(2):
-                part = work.tile([P, S], F32, name="part", bufs=4)
+                part = new_tile("pt%d%d" % (half, r), [P, S], F32)
                 nc.vector.tensor_tensor(
                     part[:], y_own[:].indirect(pos_lists[r][:, half * LCOL : (half + 1) * LCOL]), gate_sb[:, r, tokens], MULT
                 )
@@ -196,18 +235,10 @@ def tile_moe_loc_glu_relu_kernel(tc, x_words, x_scales, xo, w1_words, w1_scales,
             nc.vector.tensor_tensor(total[:], parts[0][:], parts[1][:], ADD)
             nc.sync.dma_start(out=out[:, tokens], in_=total[:])
 
-        count = len(UNITS)
-        gather(0)
-        gather(1)
-        cast_own_tokens()
-        for step in range(count + 2):
-            if step < count:
-                first_layer(step)
-            if 1 <= step <= count:
-                turn(step - 1)
-            if step >= 2:
-                second_layer(step - 2)
-            if step + 2 < count:
-                gather(step + 2)
-        combine(0)
-        combine(1)
+        steps = {"gw": gather_words, "gb": gather_bytes, "go": gather_own, "il": interleave, "qx": quantize_own,
+                 "F": first_layer, "T": turn, "S": second_layer, "C": combine}
+        for token in ORDER:
+            if token == "cast":
+                cast_own_tokens()
+            else:
+                steps[token[:-1]](int(token[-1]))

@@ -19,13 +19,14 @@ ADD = mybir.AluOpType.add
 RELU = mybir.ActivationFunctionType.Relu
 
 P = 128
+BANK = 2048
 PAIR = 2
 S = PAIR * C
 LCOL = S // 16
 UNITS = [("far", 0), ("own", 0), ("own", 1), ("own", 2), ("own", 3), ("far", 1), ("far", 2), ("far", 3)]
-REUSES = {"pk4": "r01", "xg3": "r00", "xg4": "r11", "s5": "r21", "s6": "r30", "s7": "r40", "pt10": "hg6", "pt11": "hg7", "pt00": "r71"}
-LOADS = "fl fw xr0 xs xr1 ol w3_0 w3s w1s w1_0 w2 w2s w1_1 w3_1 w1_2 w3_2 w1_3 w3_3 p0 p1 gate".split()
-ORDER = "cast gw0 gb0 gw5 gw6 gw7 go1 il1 qx1 go2 il2 qx2 go3 F0 go4 il3 qx3 F1 T0 il4 qx4 F2 T1 S0 gb5 F3 T2 S1 gb6 F4 T3 S2 gb7 F5 T4 S3 F6 S4 T5 F7 T6 S5 T7 S6 S7 C0 C1".split()
+REUSES = {"xg3": "r00", "s5": "r30", "s6": "r21", "s7": "r10", "pt10": "r70", "pt11": "hg7", "pt00": "r20", "pt01": "r70", "c6": "r40"}
+LOADS = "fl fw xr0 xs ol xr1 w1_0 w2s w1_3 w1s w3_0 w3s p0 w3_1 w3_2 w1_1 w1_2 w2 gate p1 w3_3".split()
+ORDER = "gw0 gb0 cast go1 iv1 F0 go2 go4 qx1 F1 gw7 T0 iv4 il2 go3 qx2 F2 il3 qx3 T1 F3 qx4 S0 S1 gb6 T2 gw5 F4 gw6 gb7 gb5 T3 S2 F5 T4 F6 S3 S4 F7 T7 T5 T6 S5 S7 C0 S6 C1".split()
 STEPPED = False
 
 
@@ -110,7 +111,8 @@ def tile_moe_loc_glu_relu_kernel(tc, x_words, x_scales, xo, w1_words, w1_scales,
         def new_tile(name, shape, dtype):
             home = REUSES.get(name, name)
             if home in offsets:
-                return placed.tile(shape, dtype, name=name, align_bytes=64, offset=offsets[home])
+                beside = 1024 * [t for t in REUSES if REUSES[t] == home].index(name) if name in REUSES else 0
+                return placed.tile(shape, dtype, name=name, align_bytes=64, offset=offsets[home] + beside)
             return keep.tile(shape, dtype, name=name, align_bytes=64)
 
         h_rows = {}
@@ -147,10 +149,16 @@ def tile_moe_loc_glu_relu_kernel(tc, x_words, x_scales, xo, w1_words, w1_scales,
             for u in range(2):
                 nc.vector.tensor_copy(dst[u], xo_pairs[u][:].rearrange("p t e -> p (t e)").bitcast(U32).indirect(own_list[:, list_cols(n)]))
 
-        def interleave(n):
+        def interleave(n, on_vector=False):
             if STEPPED:
                 return
             x_grouped[n] = new_tile("xg%d" % n, [P, S * 4], BF16)
+            if on_vector:
+                nc.vector.tensor_copy(
+                    out=x_grouped[n][:].bitcast(I32).rearrange("p (s u) -> p s u", u=2),
+                    in_=picked[n][:].bitcast(I32).rearrange("p u s -> p s u"),
+                )
+                return
             nc.scalar.copy(
                 out=x_grouped[n][:].rearrange("p (s u e) -> p s u e", u=2, e=2),
                 in_=picked[n][:].rearrange("p u (s e) -> p s u e", e=2),
@@ -167,8 +175,9 @@ def tile_moe_loc_glu_relu_kernel(tc, x_words, x_scales, xo, w1_words, w1_scales,
             h_rows[n] = []
             for i in range(PAIR):
                 slots = slice(i * C, (i + 1) * C)
-                a = psum.tile([P, H], F32, name="a_bank", bufs=3)
-                b = psum.tile([P, H], F32, name="b_bank", bufs=2)
+                a = psum.tile([P, H], F32, name="a%d%d" % (n, i), offset=BANK * ((2 * n + i) % 3))
+                b_bank = 3 + n % 1 if i == 0 else 4 + n % 4
+                b = psum.tile([P, H], F32, name="b%d%d" % (n, i), offset=BANK * b_bank)
                 for bank, w_sb, plane in ((a, w1_sb, w1_plane), (b, w3_sb, w3_plane)):
                     nc.tensor.matmul_mx(
                         out=bank[:],
@@ -181,12 +190,12 @@ def tile_moe_loc_glu_relu_kernel(tc, x_words, x_scales, xo, w1_words, w1_scales,
                     )
                 relu_a = new_tile("r%d%d" % (n, i), [P, 2, P, 2], F32)
                 nc.scalar.activation(relu_a[:], a[:].rearrange("s (p u e) -> s u p e", u=2, e=2), RELU)
-                h = work.tile([P, 2, P, 2], BF16, name="h_rows", bufs=4, align_bytes=64)
+                h = work.tile([P, 2, P, 2], BF16, name="h_rows", bufs=16, align_bytes=64)
                 nc.vector.tensor_tensor(h[:], relu_a[:], b[:].rearrange("s (p u e) -> s u p e", u=2, e=2), MULT)
                 h_rows[n].append(h)
 
         def turn(n):
-            turned = psum.tile([P, PAIR, 2, C], F32, name="turned", bufs=2)
+            turned = psum.tile([P, PAIR, 2, C], F32, name="turned%d" % n, offset=BANK * (4 + n % 4))
             for i in range(PAIR):
                 for u in range(2):
                     nc.tensor.transpose(turned[:, i, u, :], h_rows[n][i][:, u].rearrange("s p e -> s (p e)").bitcast(F32), ident[:])
@@ -203,7 +212,7 @@ def tile_moe_loc_glu_relu_kernel(tc, x_words, x_scales, xo, w1_words, w1_scales,
         def second_layer(n):
             kind, j = UNITS[n]
             codes, scales = h_mx[n]
-            y = psum.tile([P, S], F32, name="y_bank", bufs=1)
+            y = psum.tile([P, S], F32, name="y%d" % n, offset=BANK * (4 + n % 4))
             for i in range(PAIR):
                 slots = slice(i * C, (i + 1) * C)
                 nc.tensor.matmul_mx(
@@ -235,7 +244,7 @@ def tile_moe_loc_glu_relu_kernel(tc, x_words, x_scales, xo, w1_words, w1_scales,
             nc.vector.tensor_tensor(total[:], parts[0][:], parts[1][:], ADD)
             nc.sync.dma_start(out=out[:, tokens], in_=total[:])
 
-        steps = {"gw": gather_words, "gb": gather_bytes, "go": gather_own, "il": interleave, "qx": quantize_own,
+        steps = {"gw": gather_words, "gb": gather_bytes, "go": gather_own, "il": interleave, "iv": lambda n: interleave(n, True), "qx": quantize_own,
                  "F": first_layer, "T": turn, "S": second_layer, "C": combine}
         for token in ORDER:
             if token == "cast":

from contextlib import ExitStack

import concourse.mybir as mybir
from concourse.masks import make_identity

K, T, Q, E, C, H, N = 512, 512, 1024, 8, 128, 512, 128
FLOPS = 2 * (2 * E * C) * (2 * K * H + H * N)

F32 = mybir.dt.float32
BF16 = mybir.dt.bfloat16
I32 = mybir.dt.int32
U32 = mybir.dt.uint32
U16 = mybir.dt.uint16
U8 = mybir.dt.uint8
FP8X4 = mybir.dt.float8_e4m3fn_x4
FP4X4 = mybir.dt.float4_e2m1fn_x4
MULT = mybir.AluOpType.mult
ADD = mybir.AluOpType.add
RELU = mybir.ActivationFunctionType.Relu

P = 128
BANK = 2048
PAIR = 2
S = PAIR * C
LCOL = S // 16
UNITS = [("far", 0), ("own", 0), ("own", 1), ("own", 2), ("own", 3), ("far", 1), ("far", 2), ("far", 3)]
REUSES = {"xg3": "r00", "s5": "r30", "s6": "r21", "s7": "r10", "pt10": "r70", "pt11": "hg7", "pt00": "r20", "pt01": "r70", "c6": "r40"}
LOADS = "fl fw xr0 xs ol xr1 w1_0 w2s w1_3 w1s w3_0 w3s p0 w3_1 w3_2 w1_1 w1_2 w2 gate p1 w3_3".split()
ORDER = "gw0 gb0 cast go1 iv1 F0 go2 go4 qx1 F1 gw7 T0 iv4 il2 go3 qx2 F2 il3 qx3 T1 F3 qx4 S0 S1 gb6 T2 gw5 F4 gw6 gb7 gb5 T3 S2 F5 T4 F6 S3 S4 F7 T7 T5 T6 S5 S7 C0 S6 C1".split()
STEPPED = False


def tile_moe_loc_glu_relu_kernel(tc, x_words, x_scales, xo, w1_words, w1_scales, w3_words, w3_scales, w2_words, w2_scales, gate, offs, pos1, pos2, offs2, out):
    nc = tc.nc
    with ExitStack() as ctx:
        lists = ctx.enter_context(tc.tile_pool(name="lists", bufs=1))
        keep = ctx.enter_context(tc.tile_pool(name="keep", bufs=1))
        work = ctx.enter_context(tc.tile_pool(name="work", bufs=3))
        placed = ctx.enter_context(tc.tile_pool(name="placed", bufs=1))
        psum = ctx.enter_context(tc.psum_pool(name="psum", bufs=1))

        own_list = lists.tile([P, E * C // 16], U16, name="own_list")
        far_list = lists.tile([P, E * C // 16], U16, name="far_list")
        pos_lists = [lists.tile([P, T // 16], U16, name="pos_list%d" % r) for r in range(2)]

        far_words = keep.tile([P, Q], I32, name="far_words", align_bytes=64)
        far_bytes = keep.tile([P, Q], U8, name="far_bytes", align_bytes=64)
        w1_plane = keep.tile([P, E, H], U8, name="w1_plane", align_bytes=64)
        w3_plane = keep.tile([P, E, H], U8, name="w3_plane", align_bytes=64)
        w2_plane = keep.tile([P, E, N], U8, name="w2_plane", align_bytes=64)
        w1_sb = [keep.tile([P, PAIR, 2 * H], U8, name="w1_sb%d" % j, align_bytes=64) for j in range(E // PAIR)]
        w3_sb = [keep.tile([P, PAIR, 2 * H], U8, name="w3_sb%d" % j, align_bytes=64) for j in range(E // PAIR)]
        w2_sb = keep.tile([P, E, 2 * N], U8, name="w2_sb", align_bytes=64)
        xo_raw = [keep.tile([P, 2, T], F32, name="xo_raw%d" % u) for u in range(2)]
        xo_pairs = [keep.tile([P, T, 2], BF16, name="xo_pairs%d" % u, align_bytes=64) for u in range(2)]
        gate_sb = keep.tile([P, 2, T], F32, name="gate_sb")
        y_own = keep.tile([P, E * C], F32, name="y_own")
        ident = keep.tile([P, P], F32, name="ident")

        nc.vector.memset(far_bytes[:].bitcast(I32), 0)
        nc.gpsimd.memset(w1_plane[:].bitcast(I32), 0)
        nc.vector.memset(w3_plane[:].bitcast(I32), 0)
        nc.vector.memset(w2_plane[:].bitcast(I32), 0)
        make_identity(nc, ident[:])

        def load_plane(plane, scales):
            for r in range(4):
                nc.sync.dma_start(
                    out=plane[r:P:32].bitcast(I32),
                    in_=scales[:, 0].rearrange("e (q r) i -> r q e i", r=4)[r].bitcast(I32),
                )

        def load_words(dst, words, first, count):
            nc.sync.dma_start(
                out=dst[:].bitcast(I32),
                in_=words[first : first + count, 0].rearrange("e p c -> p e c").bitcast(I32),
            )

        xo_rows = xo.rearrange("(p j) t -> p j t", j=4)

        def load(name):
            if name in ("fl", "ol", "p0", "p1"):
                dst, src = {"fl": (far_list, offs2), "ol": (own_list, offs), "p0": (pos_lists[0], pos1), "p1": (pos_lists[1], pos2)}[name]
                nc.sync.dma_start(dst[:], src)
            elif name == "fw":
                nc.sync.dma_start(out=far_words[:], in_=x_words[0].rearrange("p n d -> p (n d)").bitcast(I32))
            elif name in ("xr0", "xr1"):
                u = int(name[2])
                nc.sync.dma_start(out=xo_raw[u][:], in_=xo_rows[:, 2 * u : 2 * u + 2, :])
            elif name == "xs":
                for r in range(4):
                    nc.sync.dma_start(out=far_bytes[r:P:32].bitcast(I32), in_=x_scales[0].rearrange("(q r) n -> r q n", r=4)[r].bitcast(I32))
            elif name in ("w1s", "w3s", "w2s"):
                load_plane(*{"w1s": (w1_plane, w1_scales), "w3s": (w3_plane, w3_scales), "w2s": (w2_plane, w2_scales)}[name])
            elif name == "w2":
                load_words(w2_sb, w2_words, 0, E)
            elif name == "gate":
                nc.sync.dma_start(out=gate_sb[:], in_=gate.rearrange("r p t -> p r t"))
            else:
                j = int(name[3])
                load_words((w1_sb if name[1] == "1" else w3_sb)[j], w1_words if name[1] == "1" else w3_words, PAIR * j, PAIR)

        for name in LOADS:
            load(name)

        SLOT = 2048
        offsets = {"r%d%d" % (n, i): SLOT * (2 * n + i) for n in range(8) for i in range(2)}
        for n in range(8):
            offsets["hg%d" % n] = SLOT * (16 + n)

        def new_tile(name, shape, dtype):
            home = REUSES.get(name, name)
            if home in offsets:
                beside = 1024 * [t for t in REUSES if REUSES[t] == home].index(name) if name in REUSES else 0
                return placed.tile(shape, dtype, name=name, align_bytes=64, offset=offsets[home] + beside)
            return keep.tile(shape, dtype, name=name, align_bytes=64)

        h_rows = {}
        h_mx = {}

        def cast_own_tokens():
            for u in range(2):
                nc.scalar.copy(out=xo_pairs[u][:], in_=xo_raw[u][:].rearrange("p e t -> p t e"))

        x_codes = {}
        x_bytes = {}
        picked = {}
        x_grouped = {}

        def list_cols(n):
            j = UNITS[n][1]
            return slice(j * LCOL, (j + 1) * LCOL)

        def gather_words(n):
            x_codes[n] = new_tile("c%d" % n, [P, S], U32)
            nc.vector.tensor_copy(x_codes[n][:], far_words[:].bitcast(U32).indirect(far_list[:, list_cols(n)]))

        def gather_bytes(n):
            x_bytes[n] = new_tile("s%d" % n, [P, S], U8)
            nc.vector.tensor_copy(x_bytes[n][:], far_bytes[:].indirect(far_list[:, list_cols(n)]))

        def gather_own(n):
            if STEPPED:
                x_grouped[n] = new_tile("xg%d" % n, [P, S * 4], BF16)
                dst = [x_grouped[n][:].bitcast(U32).rearrange("p (s u) -> p s u", u=2)[:, :, u] for u in range(2)]
            else:
                picked[n] = new_tile("pk%d" % n, [P, 2, S * 2], BF16)
                dst = [picked[n][:, u].bitcast(U32) for u in range(2)]
            for u in range(2):
                nc.vector.tensor_copy(dst[u], xo_pairs[u][:].rearrange("p t e -> p (t e)").bitcast(U32).indirect(own_list[:, list_cols(n)]))

        def interleave(n, on_vector=False):
            if STEPPED:
                return
            x_grouped[n] = new_tile("xg%d" % n, [P, S * 4], BF16)
            if on_vector:
                nc.vector.tensor_copy(
                    out=x_grouped[n][:].bitcast(I32).rearrange("p (s u) -> p s u", u=2),
                    in_=picked[n][:].bitcast(I32).rearrange("p u s -> p s u"),
                )
                return
            nc.scalar.copy(
                out=x_grouped[n][:].rearrange("p (s u e) -> p s u e", u=2, e=2),
                in_=picked[n][:].rearrange("p u (s e) -> p s u e", e=2),
            )

        def quantize_own(n):
            x_codes[n] = new_tile("c%d" % n, [P, S], U32)
            x_bytes[n] = new_tile("s%d" % n, [P, S], U8)
            nc.vector.quantize_mx(out=x_codes[n][:].bitcast(FP8X4), scales=x_bytes[n][:], in_=x_grouped[n][:])

        def first_layer(n):
            kind, j = UNITS[n]
            codes, scales = x_codes[n], x_bytes[n]
            h_rows[n] = []
            for i in range(PAIR):
                slots = slice(i * C, (i + 1) * C)
                a = psum.tile([P, H], F32, name="a%d%d" % (n, i), offset=BANK * ((2 * n + i) % 3))
                b_bank = 3 + n % 1 if i == 0 else 4 + n % 4
                b = psum.tile([P, H], F32, name="b%d%d" % (n, i), offset=BANK * b_bank)
                for bank, w_sb, plane in ((a, w1_sb, w1_plane), (b, w3_sb, w3_plane)):
                    nc.tensor.matmul_mx(
                        out=bank[:],
                        lhsT=codes[:, slots].bitcast(FP8X4),
                        lhsT_scale=scales[:, slots],
                        rhs=w_sb[j][:, i, :].bitcast(FP4X4),
                        rhs_scale=plane[:, PAIR * j + i, :],
                        start=True,
                        stop=True,
                    )
                relu_a = new_tile("r%d%d" % (n, i), [P, 2, P, 2], F32)
                nc.scalar.activation(relu_a[:], a[:].rearrange("s (p u e) -> s u p e", u=2, e=2), RELU)
                h = work.tile([P, 2, P, 2], BF16, name="h_rows", bufs=16, align_bytes=64)
                nc.vector.tensor_tensor(h[:], relu_a[:], b[:].rearrange("s (p u e) -> s u p e", u=2, e=2), MULT)
                h_rows[n].append(h)

        def turn(n):
            turned = psum.tile([P, PAIR, 2, C], F32, name="turned%d" % n, offset=BANK * (4 + n % 4))
            for i in range(PAIR):
                for u in range(2):
                    nc.tensor.transpose(turned[:, i, u, :], h_rows[n][i][:, u].rearrange("s p e -> s (p e)").bitcast(F32), ident[:])
            grouped = new_tile("hg%d" % n, [P, S * 4], BF16)
            nc.scalar.copy(
                out=grouped[:].bitcast(F32).rearrange("p (i s u) -> p i s u", i=PAIR, u=2),
                in_=turned[:].rearrange("p i u s -> p i s u"),
            )
            codes = work.tile([P, S], U32, name="h_codes", align_bytes=64)
            scales = work.tile([P, S], U8, name="h_bytes", align_bytes=64)
            nc.vector.quantize_mx(out=codes[:].bitcast(FP8X4), scales=scales[:], in_=grouped[:])
            h_mx[n] = (codes, scales)

        def second_layer(n):
            kind, j = UNITS[n]
            codes, scales = h_mx[n]
            y = psum.tile([P, S], F32, name="y%d" % n, offset=BANK * (4 + n % 4))
            for i in range(PAIR):
                slots = slice(i * C, (i + 1) * C)
                nc.tensor.matmul_mx(
                    out=y[:, slots],
                    lhsT=w2_sb[:, PAIR * j + i, :].bitcast(FP4X4),
                    lhsT_scale=w2_plane[:, PAIR * j + i, :],
                    rhs=codes[:, slots].bitcast(FP8X4),
                    rhs_scale=scales[:, slots],
                    start=True,
                    stop=True,
                )
            if kind == "own":
                nc.scalar.copy(out=y_own[:, j * S : (j + 1) * S], in_=y[:])
                return
            z = work.tile([P, S], F32, name="z")
            nc.scalar.copy(out=z[:], in_=y[:])
            nc.sync.dma_start(out=out[:, T + j * S : T + (j + 1) * S], in_=z[:])

        def combine(half):
            tokens = slice(half * S, (half + 1) * S)
            parts = []
            for r in range(2):
                part = new_tile("pt%d%d" % (half, r), [P, S], F32)
                nc.vector.tensor_tensor(
                    part[:], y_own[:].indirect(pos_lists[r][:, half * LCOL : (half + 1) * LCOL]), gate_sb[:, r, tokens], MULT
                )
                parts.append(part)
            total = work.tile([P, S], F32, name="total")
            nc.vector.tensor_tensor(total[:], parts[0][:], parts[1][:], ADD)
            nc.sync.dma_start(out=out[:, tokens], in_=total[:])

        steps = {"gw": gather_words, "gb": gather_bytes, "go": gather_own, "il": interleave, "iv": lambda n: interleave(n, True), "qx": quantize_own,
                 "F": first_layer, "T": turn, "S": second_layer, "C": combine}
        for token in ORDER:
            if token == "cast":
                cast_own_tokens()
            else:
                steps[token[:-1]](int(token[-1]))
